import numpy as np
import ml_dtypes


def mxq(x, axis, fmt="e4m3"):
    dtype, down = {"e4m3": (ml_dtypes.float8_e4m3fn, 7), "e5m2": (ml_dtypes.float8_e5m2, 14)}[fmt]
    v = np.moveaxis(np.asarray(x, np.float32).astype(ml_dtypes.bfloat16).astype(np.float64), axis, -1)
    blocks = v.reshape(v.shape[:-1] + (-1, 32))
    amax = np.abs(blocks).max(-1, keepdims=True)
    byte = np.maximum(np.where(amax > 0, np.frexp(amax)[1] - 1 + 127, 0) - down, 1)
    scale = np.exp2(byte - 127.0)
    codes = (blocks / scale).astype(np.float32).astype(dtype).astype(np.float64)
    return np.moveaxis((codes * scale).reshape(v.shape), -1, axis)


WIDE = False


def mx_kscale(k):
    if not WIDE:
        return np.ones(k)
    levels = np.array([30, -30])
    if k % 512:
        return np.exp2(np.random.permutation(np.resize(levels, k // 32))).repeat(32)
    a = np.empty((k // 512, 16))
    for p in range(k // 512):
        a[p, :8] = np.random.permutation(np.resize(levels, 8))
        for g in range(8):
            far = levels[np.abs(levels - a[p, g]) >= 10]
            a[p, g + 8] = far[np.random.randint(len(far))]
    return np.exp2(a.ravel()).repeat(32)


def f64(x):
    return np.asarray(x).astype(np.float64)


def striped(idx):
    return np.tile(np.asarray(idx).reshape(-1, 16).T, (8, 1)).astype(np.uint16)


def unstriped(offs):
    return offs[:16].T.reshape(-1).astype(np.int64)


E2M1 = np.array([0.0, 0.5, 1.0, 1.5, 2.0, 3.0, 4.0, 6.0, -0.0, -0.5, -1.0, -1.5, -2.0, -3.0, -4.0, -6.0])


def pack_weight(w, fmt):
    k, n = w.shape
    w = f64(np.asarray(w, np.float32).astype(ml_dtypes.bfloat16)).reshape(k // 32, 32, n)
    amax = np.abs(w).max(1)
    if fmt in ("e4m3", "e5m2"):
        byte = np.frexp(amax)[1] - 1 + 127 - (7 if fmt == "e4m3" else 14)
    else:
        mant, ex = np.frexp(amax / 6.0)
        byte = np.where(mant > 0.5, ex, ex - 1) + 127
    byte = np.clip(np.where(amax > 0, byte, 1), 1, 254)
    scaled = (w * np.exp2(127.0 - byte)[:, None, :]).reshape(k, n).astype(np.float32)
    by_word = np.ascontiguousarray(scaled.reshape(k // 512, 128, 4, n).transpose(0, 1, 3, 2))
    if fmt in ("e4m3", "e5m2"):
        words = by_word.astype(ml_dtypes.float8_e4m3fn if fmt == "e4m3" else ml_dtypes.float8_e5m2).view(np.uint8)
    else:
        c = by_word.astype(ml_dtypes.float4_e2m1fn).view(np.uint8) & 0xF
        words = (c[..., 0::2] | (c[..., 1::2] << 4)).reshape(k // 512, 128, 2 * n)
    return np.ascontiguousarray(words), np.ascontiguousarray(byte.astype(np.uint8).reshape(k // 512, 16, n))


def unpack_weight(words, scales, fmt):
    g, _, n = scales.shape
    words = np.ascontiguousarray(words).reshape(g, 128, n, -1)
    if fmt in ("e4m3", "e5m2"):
        vals = words.view(ml_dtypes.float8_e4m3fn if fmt == "e4m3" else ml_dtypes.float8_e5m2).astype(np.float64)
    else:
        nib = np.empty((g, 128, n, 4), np.uint8)
        nib[..., 0::2] = words & 0xF
        nib[..., 1::2] = words >> 4
        vals = E2M1[nib]
    vals = vals * np.repeat(np.exp2(scales.astype(np.float64) - 127.0), 8, axis=1)[..., None]
    return vals.transpose(0, 1, 3, 2).reshape(g * 512, n)


def sigmoid(v):
    return 1.0 / (1.0 + np.exp(-v))


def sgn(shape):
    return np.random.uniform(0.5, 2.0, shape) * np.where(np.random.standard_normal(shape) < 0, -1.0, 1.0)


K, T, J, R, F, Z, I, O, N, E = 512, 1024, 256, 512, 512, 1024, 256, 128, 256, 1024


def setup_inputs():
    n = np.random.standard_normal
    idx = np.random.permutation(T)[:J]
    idx2 = np.random.permutation(Z)[:J]
    idx3 = np.random.permutation(J)[:I]
    idx4 = np.random.permutation(J)[:I]
    idx5 = np.random.permutation(T)[:O]
    idx6 = np.random.permutation(E)[:O]
    fk = mx_kscale(K)
    ff = mx_kscale(F)
    fr = mx_kscale(R)
    xtp = pack_weight(n((K, T)) / fk[:, None], "e4m3")
    xop = pack_weight(n((F, Z)) / ff[:, None], "e2m1")
    wp = pack_weight(n((K, R)) * 1 / np.sqrt(K) * fk[:, None], "e2m1")
    w0p = pack_weight(n((F, R)) * 1 / np.sqrt(F) * ff[:, None], "e5m2")
    wbp = pack_weight(n((R, N)) * 1 / np.sqrt(R) / fr[:, None], "e5m2")
    wsp = pack_weight(n((K, N)) * 1 / np.sqrt(K) * fk[:, None], "e5m2")
    return {
        "xt_words": xtp[0],
        "xt_scales": xtp[1],
        "xo_words": xop[0],
        "xo_scales": xop[1],
        "w_words": wp[0],
        "w_scales": wp[1],
        "w0_words": w0p[0],
        "w0_scales": w0p[1],
        "sa": (sgn((R, 1)) * fr[:, None]).astype(np.float32),
        "sg": (sgn((R, 1))).astype(np.float32),
        "bg": (np.random.uniform(-2.0, 2.0, (R, 1))).astype(np.float32),
        "wb_words": wbp[0],
        "wb_scales": wbp[1],
        "ws_words": wsp[0],
        "ws_scales": wsp[1],
        "offs": striped(idx),
        "offs2": striped(idx2),
        "offs3": striped(idx3),
        "offs4": striped(idx4),
        "offs5": striped(idx5),
        "offs6": striped(idx6),
    }


def reference(xt_words, xt_scales, xo_words, xo_scales, w_words, w_scales, w0_words, w0_scales, sa, sg, bg, wb_words, wb_scales, ws_words, ws_scales, offs, offs2, offs3, offs4, offs5, offs6):
    idx = unstriped(offs)
    idx2 = unstriped(offs2)
    idx3 = unstriped(offs3)
    idx4 = unstriped(offs4)
    idx5 = unstriped(offs5)
    idx6 = unstriped(offs6)
    xtu = unpack_weight(xt_words, xt_scales, "e4m3")
    xou = unpack_weight(xo_words, xo_scales, "e2m1")
    wu = unpack_weight(w_words, w_scales, "e2m1")
    w0u = unpack_weight(w0_words, w0_scales, "e5m2")
    wbu = unpack_weight(wb_words, wb_scales, "e5m2")
    wsu = unpack_weight(ws_words, ws_scales, "e5m2")
    xtidxg = xtu[:, idx]
    xoidx2g = xou[:, idx2]
    a = wu.T @ xtidxg + w0u.T @ xoidx2g
    h1 = a[:, idx3] * f64(sa) * sigmoid(a[:, idx4] * f64(sg) + f64(bg))
    hid = h1.reshape(R, O, I // O).max(axis=2)
    hidq = mxq(hid, 0, "e4m3")
    xtidx5g = xtu[:, idx5]
    p = wbu.T @ hidq + wsu.T @ xtidx5g
    y = np.zeros((N, E))
    y[:, idx6] = p
    return y

@@ -1,0 +1,209 @@
+from contextlib import ExitStack
+
+import concourse.mybir as mybir
+
+K, T, J, R, F, Z, I, O, N, E = 512, 1024, 256, 512, 512, 1024, 256, 128, 256, 1024
+FLOPS = 2 * (K * R * J + F * R * J + R * N * O + K * N * O)
+
+F32 = mybir.dt.float32
+BF16 = mybir.dt.bfloat16
+I32 = mybir.dt.int32
+U32 = mybir.dt.uint32
+U16 = mybir.dt.uint16
+U8 = mybir.dt.uint8
+E4M3 = mybir.dt.float8_e4m3fn_x4
+E5M2 = mybir.dt.float8_e5m2_x4
+E2M1 = mybir.dt.float4_e2m1fn_x4
+ACT = mybir.ActivationFunctionType
+ALU = mybir.AluOpType
+
+P = 128
+PACK = 4
+HALVES = 2
+PICKS = I // HALVES
+POOLS = O // HALVES
+
+
+def fp8_words(words):
+    return words[0].rearrange("p c b -> p (c b)").bitcast(I32)
+
+
+def scale_rows(scales, q):
+    return scales[0].rearrange("(h q r) c -> q r h c", h=2, q=2)[q].bitcast(I32)
+
+
+def tile_list_gatedpool_bank_further_scattered_kernel(
+    tc, xt_words, xt_scales, xo_words, xo_scales, w_words, w_scales, w0_words, w0_scales, sa, sg, bg,
+    wb_words, wb_scales, ws_words, ws_scales, offs, offs2, offs3, offs4, offs5, offs6, out,
+):
+    nc = tc.nc
+    with ExitStack() as ctx:
+        keep = ctx.enter_context(tc.tile_pool(name="keep", bufs=1))
+        psum = ctx.enter_context(tc.psum_pool(name="psum", bufs=1))
+
+        def sb(name, shape, dtype):
+            return keep.tile(shape, dtype, name=name, align_bytes=64)
+
+        def load_list(name, src):
+            tile = keep.tile(list(src.shape), U16, name=name)
+            nc.sync.dma_start(tile[:], src)
+            return tile
+
+        xt_stage = sb("xt_stage", [64, 2, T], U8)
+        xo_stage = sb("xo_stage", [64, 2, Z], U8)
+        w_stage = sb("w_stage", [P, 2, 2, R], U8)
+        late_planes = sb("late_planes", [P, 2, N], U8)
+        nc.vector.memset(xt_stage[:].bitcast(I32), 0)
+        nc.vector.memset(xo_stage[:].bitcast(I32), 0)
+        nc.vector.memset(w_stage[0:64].bitcast(I32), 0)
+        nc.vector.memset(late_planes[:].bitcast(I32), 0)
+        pages = [sb(f"page{b}", [P, E], F32) for b in range(N // P)]
+        for page in pages:
+            nc.vector.memset(page[:], 0.0)
+
+        xt_w = sb("xt_w", [P, T], U32)
+        xo_w = sb("xo_w", [P, Z], U16)
+        w0_raw = sb("w0_raw", [P, R], U32)
+        w_raw = sb("w_raw", [P, R], U16)
+        nc.scalar.dma_start(xt_w[:].bitcast(I32), fp8_words(xt_words))
+        nc.scalar.dma_start(xo_w[:].bitcast(I32), xo_words[0].bitcast(I32))
+        nc.scalar.dma_start(w0_raw[:].bitcast(I32), fp8_words(w0_words))
+        nc.scalar.dma_start(w_raw[:].bitcast(I32), w_words[0].bitcast(I32))
+
+        list1 = load_list("list1", offs)
+        for q in range(2):
+            nc.sync.dma_start(xt_stage[32 * q : 32 * q + 4].bitcast(I32), scale_rows(xt_scales, q))
+        list2 = load_list("list2", offs2)
+        for q in range(2):
+            nc.sync.dma_start(xo_stage[32 * q : 32 * q + 4].bitcast(I32), scale_rows(xo_scales, q))
+        for i, scales in enumerate((w_scales, w0_scales)):
+            for q in range(2):
+                nc.sync.dma_start(w_stage[32 * q : 32 * q + 4, :, i, :].bitcast(I32), scale_rows(scales, q))
+        list4 = load_list("list4", offs4)
+        list3 = load_list("list3", offs3)
+
+        rowvals = []
+        for name, src in (("sg_t", sg), ("bg_t", bg), ("sa_t", sa)):
+            tile = keep.tile([P, PACK], F32, name=name)
+            nc.gpsimd.dma_start(tile[:], src.rearrange("(p t) one -> p (t one)", t=PACK))
+            rowvals.append(tile)
+        sg_t, bg_t, sa_t = rowvals
+
+        list5 = load_list("list5", offs5)
+        ws_w = sb("ws_w", [P, N], U32)
+        wb_w = sb("wb_w", [P, N], U32)
+        nc.sync.dma_start(ws_w[:].bitcast(I32), fp8_words(ws_words))
+        nc.sync.dma_start(wb_w[:].bitcast(I32), fp8_words(wb_words))
+        for i, scales in enumerate((ws_scales, wb_scales)):
+            for q in range(4):
+                nc.sync.dma_start(
+                    late_planes[32 * q : 32 * q + 4, i, :].bitcast(I32), scales[0, 4 * q : 4 * q + 4, :].bitcast(I32)
+                )
+        list6 = load_list("list6", offs6)
+
+        def spread(name, stage, width):
+            plane = sb(name, [P, width], U8)
+            for h in range(2):
+                nc.vector.tensor_copy(plane[64 * h : 64 * h + 64, :].bitcast(I32), stage[:, h, :].bitcast(I32))
+            return plane
+
+        def gather(name, window, lst, dtype):
+            dense = sb(name, [P, 16 * lst.shape[1]], dtype)
+            nc.vector.tensor_copy(dense[:], window[:].indirect(lst[:]))
+            return dense
+
+        xt_s = spread("xt_s", xt_stage, T)
+        tok_s = gather("tok_s", xt_s, list1, U8)
+        tok_w = gather("tok_w", xt_w, list1, U32)
+        note_w = gather("note_w", xo_w, list2, U16)
+        xo_s = spread("xo_s", xo_stage, Z)
+        note_s = gather("note_s", xo_s, list2, U8)
+
+        w0_w = sb("w0_w", [P, R], U32)
+        w_w = sb("w_w", [P, R], U16)
+        nc.scalar.copy(
+            w0_w[:].rearrange("p (t c i) -> p c t i", t=PACK, i=4),
+            w0_raw[:].rearrange("p (c i t) -> p c t i", t=PACK, i=4),
+        )
+        nc.scalar.copy(
+            w_w[:].rearrange("p (t m) -> p t m", t=PACK), w_raw[:].rearrange("p (m t) -> p t m", t=PACK)
+        )
+        nc.vector.tensor_copy(
+            w_stage[64:128, 0].rearrange("p i c -> p (i c)").bitcast(I32),
+            w_stage[0:64, 1].rearrange("p i c -> p (i c)").bitcast(I32),
+        )
+        w_planes = sb("w_planes", [P, 2, R], U8)
+        nc.vector.tensor_copy(
+            w_planes[:].rearrange("p i (t m) -> p i t m", t=PACK),
+            w_stage[:, 0].rearrange("p i (m t) -> p i t m", t=PACK),
+        )
+
+        banks = [psum.tile([P, J], F32, name=f"a_bank{t}") for t in range(PACK)]
+        for t in range(PACK):
+            cols = slice(P * t, P * (t + 1))
+            nc.tensor.matmul_mx(
+                banks[t][:], lhsT=w_w[:, cols].bitcast(E2M1), lhsT_scale=w_planes[:, 0, cols],
+                rhs=tok_w[:].bitcast(E4M3), rhs_scale=tok_s[:], start=True, stop=False,
+            )
+        a_rows = []
+        for t in range(PACK):
+            cols = slice(P * t, P * (t + 1))
+            nc.tensor.matmul_mx(
+                banks[t][:], lhsT=w0_w[:, cols].bitcast(E5M2), lhsT_scale=w_planes[:, 1, cols],
+                rhs=note_w[:].bitcast(E2M1), rhs_scale=note_s[:], start=False, stop=True,
+            )
+            a_t = sb(f"a_rows{t}", [P, J], F32)
+            nc.vector.tensor_copy(a_t[:], banks[t][:])
+            a_rows.append(a_t)
+
+        short_w = gather("short_w", xt_w, list5, U32)
+        short_s = gather("short_s", xt_s, list5, U8)
+        p_banks = [psum.tile([P, O], F32, name=f"p_bank{b}") for b in range(N // P)]
+        for b in range(N // P):
+            cols = slice(P * b, P * (b + 1))
+            nc.tensor.matmul_mx(
+                p_banks[b][:], lhsT=ws_w[:, cols].bitcast(E5M2), lhsT_scale=late_planes[:, 0, cols],
+                rhs=short_w[:].bitcast(E4M3), rhs_scale=short_s[:], start=True, stop=False,
+            )
+
+        hid = sb("hid", [P, O * PACK], BF16)
+        hid_w = sb("hid_w", [P, O], U32)
+        hid_s = sb("hid_s", [P, O], U8)
+        for h in range(HALVES):
+            part = slice(h * PICKS // 16, (h + 1) * PICKS // 16)
+            gates = sb(f"gates{h}", [P, PACK, PICKS], F32)
+            scaled = sb(f"scaled{h}", [P, PACK, PICKS], F32)
+            h1 = sb(f"h1_{h}", [P, PACK, PICKS], F32)
+            for t in range(PACK):
+                nc.scalar.activation(
+                    out=gates[:, t, :], in_=a_rows[t][:].indirect(list4[:, part]), func=ACT.Sigmoid,
+                    bias=bg_t[:, t : t + 1], scale=sg_t[:, t : t + 1],
+                )
+                nc.scalar.activation(
+                    out=scaled[:, t, :], in_=a_rows[t][:].indirect(list3[:, part]), func=ACT.Copy,
+                    scale=sa_t[:, t : t + 1],
+                )
+                nc.vector.tensor_tensor(h1[:, t, :], scaled[:, t, :], gates[:, t, :], ALU.mult)
+            wide = slice(h * POOLS * PACK, (h + 1) * POOLS * PACK)
+            pools = slice(h * POOLS, (h + 1) * POOLS)
+            nc.vector.tensor_reduce(
+                hid[:, wide].rearrange("p (o t) -> p o t", t=PACK),
+                h1[:].rearrange("p t (o two) -> p o t two", two=2),
+                mybir.AxisListType.X, ALU.max,
+            )
+            nc.vector.quantize_mx(out=hid_w[:, pools].bitcast(E4M3), scales=hid_s[:, pools], in_=hid[:, wide])
+
+        for b in range(N // P):
+            cols = slice(P * b, P * (b + 1))
+            nc.tensor.matmul_mx(
+                p_banks[b][:], lhsT=wb_w[:, cols].bitcast(E5M2), lhsT_scale=late_planes[:, 1, cols],
+                rhs=hid_w[:].bitcast(E4M3), rhs_scale=hid_s[:], start=False, stop=True,
+            )
+        p0 = sb("p0", [P, O], F32)
+        p1 = sb("p1", [P, O], F32)
+        nc.vector.tensor_copy(p0[:], p_banks[0][:])
+        nc.vector.tensor_copy(pages[0][:].indirect(list6[:]), p0[:])
+        nc.scalar.copy(p1[:], p_banks[1][:])
+        nc.scalar.activation(out=pages[1][:].indirect(list6[:]), in_=p1[:], func=ACT.Copy)
+        nc.sync.dma_start(out[0:P, :], pages[0][:])
+        nc.sync.dma_start(out[P : 2 * P, :], pages[1][:])

@@ -19,17 +19,11 @@ ALU = mybir.AluOpType
 
 P = 128
 PACK = 4
-HALVES = 2
-PICKS = I // HALVES
-POOLS = O // HALVES
+HALF = P // 2
 
 
 def fp8_words(words):
     return words[0].rearrange("p c b -> p (c b)").bitcast(I32)
-
-
-def scale_rows(scales, q):
-    return scales[0].rearrange("(h q r) c -> q r h c", h=2, q=2)[q].bitcast(I32)
 
 
 def tile_list_gatedpool_bank_further_scattered_kernel(
@@ -41,44 +35,52 @@ def tile_list_gatedpool_bank_further_scattered_kernel(
         keep = ctx.enter_context(tc.tile_pool(name="keep", bufs=1))
         psum = ctx.enter_context(tc.psum_pool(name="psum", bufs=1))
 
-        def sb(name, shape, dtype):
-            return keep.tile(shape, dtype, name=name, align_bytes=64)
+        def sb(name, shape, dtype, tag=None):
+            return keep.tile(shape, dtype, name=name, tag=tag or name, align_bytes=64)
 
         def load_list(name, src):
             tile = keep.tile(list(src.shape), U16, name=name)
             nc.sync.dma_start(tile[:], src)
             return tile
 
-        xt_stage = sb("xt_stage", [64, 2, T], U8)
-        xo_stage = sb("xo_stage", [64, 2, Z], U8)
-        w_stage = sb("w_stage", [P, 2, 2, R], U8)
-        late_planes = sb("late_planes", [P, 2, N], U8)
+        def load_stage(queue, stage, scales, base):
+            rows = scales[0].rearrange("(h q r) c -> q r h c", h=2, q=2)
+            for q in range(2):
+                first = base + 32 * q
+                queue.dma_start(stage[first : first + 4].bitcast(I32), rows[q].bitcast(I32))
+
+        def gather(name, window, lst, dtype):
+            dense = sb(name, [P, 16 * lst.shape[1]], dtype)
+            nc.vector.tensor_copy(dense[:], window[:].indirect(lst[:]))
+            return dense
+
+        xt_stage = sb("xt_stage", [HALF, 2, T], U8)
         nc.vector.memset(xt_stage[:].bitcast(I32), 0)
-        nc.vector.memset(xo_stage[:].bitcast(I32), 0)
-        nc.vector.memset(w_stage[0:64].bitcast(I32), 0)
+        xo_s = sb("xo_s", [P, Z], U8)
+        nc.vector.memset(xo_s[:].bitcast(I32), 0)
+        w_stage = sb("w_stage", [P, 2, 2, R], U8)
+        nc.vector.memset(w_stage[HALF:].bitcast(I32), 0)
+        late_planes = sb("late_planes", [P, 2, N], U8)
         nc.vector.memset(late_planes[:].bitcast(I32), 0)
-        pages = [sb(f"page{b}", [P, E], F32) for b in range(N // P)]
-        for page in pages:
-            nc.vector.memset(page[:], 0.0)
+        a_rows = [sb(f"a_rows{t}", [P, 2 * J], F32) for t in range(PACK)]
+        for a_t in a_rows:
+            nc.vector.memset(a_t[:, J:], 0.0)
 
         xt_w = sb("xt_w", [P, T], U32)
         xo_w = sb("xo_w", [P, Z], U16)
         w0_raw = sb("w0_raw", [P, R], U32)
         w_raw = sb("w_raw", [P, R], U16)
-        nc.scalar.dma_start(xt_w[:].bitcast(I32), fp8_words(xt_words))
-        nc.scalar.dma_start(xo_w[:].bitcast(I32), xo_words[0].bitcast(I32))
-        nc.scalar.dma_start(w0_raw[:].bitcast(I32), fp8_words(w0_words))
-        nc.scalar.dma_start(w_raw[:].bitcast(I32), w_words[0].bitcast(I32))
-
+        load_stage(nc.scalar, xt_stage, xt_scales, 0)
         list1 = load_list("list1", offs)
-        for q in range(2):
-            nc.sync.dma_start(xt_stage[32 * q : 32 * q + 4].bitcast(I32), scale_rows(xt_scales, q))
         list2 = load_list("list2", offs2)
-        for q in range(2):
-            nc.sync.dma_start(xo_stage[32 * q : 32 * q + 4].bitcast(I32), scale_rows(xo_scales, q))
-        for i, scales in enumerate((w_scales, w0_scales)):
-            for q in range(2):
-                nc.sync.dma_start(w_stage[32 * q : 32 * q + 4, :, i, :].bitcast(I32), scale_rows(scales, q))
+        nc.sync.dma_start(xt_w[:].bitcast(I32), fp8_words(xt_words))
+        nc.sync.dma_start(xo_w[:].bitcast(I32), xo_words[0].bitcast(I32))
+        nc.sync.dma_start(w0_raw[:].bitcast(I32), fp8_words(w0_words))
+        nc.sync.dma_start(w_raw[:].bitcast(I32), w_words[0].bitcast(I32))
+        for q in range(4):
+            nc.sync.dma_start(xo_s[32 * q : 32 * q + 4, :].bitcast(I32), xo_scales[0, 4 * q : 4 * q + 4, :].bitcast(I32))
+        for i, scales in enumerate((w0_scales, w_scales)):
+            load_stage(nc.sync, w_stage[:, :, i, :], scales, HALF)
         list4 = load_list("list4", offs4)
         list3 = load_list("list3", offs3)
 
@@ -101,22 +103,12 @@ def tile_list_gatedpool_bank_further_scattered_kernel(
                 )
         list6 = load_list("list6", offs6)
 
-        def spread(name, stage, width):
-            plane = sb(name, [P, width], U8)
-            for h in range(2):
-                nc.vector.tensor_copy(plane[64 * h : 64 * h + 64, :].bitcast(I32), stage[:, h, :].bitcast(I32))
-            return plane
-
-        def gather(name, window, lst, dtype):
-            dense = sb(name, [P, 16 * lst.shape[1]], dtype)
-            nc.vector.tensor_copy(dense[:], window[:].indirect(lst[:]))
-            return dense
-
-        xt_s = spread("xt_s", xt_stage, T)
-        tok_s = gather("tok_s", xt_s, list1, U8)
         tok_w = gather("tok_w", xt_w, list1, U32)
         note_w = gather("note_w", xo_w, list2, U16)
-        xo_s = spread("xo_s", xo_stage, Z)
+        xt_s = sb("xt_s", [P, T], U8)
+        for h in range(2):
+            nc.vector.tensor_copy(xt_s[HALF * h : HALF * (h + 1), :].bitcast(I32), xt_stage[:, h, :].bitcast(I32))
+        tok_s = gather("tok_s", xt_s, list1, U8)
         note_s = gather("note_s", xo_s, list2, U8)
 
         w0_w = sb("w0_w", [P, R], U32)
@@ -129,32 +121,27 @@ def tile_list_gatedpool_bank_further_scattered_kernel(
             w_w[:].rearrange("p (t m) -> p t m", t=PACK), w_raw[:].rearrange("p (m t) -> p t m", t=PACK)
         )
         nc.vector.tensor_copy(
-            w_stage[64:128, 0].rearrange("p i c -> p (i c)").bitcast(I32),
-            w_stage[0:64, 1].rearrange("p i c -> p (i c)").bitcast(I32),
+            w_stage[:HALF, 1].rearrange("p i c -> p (i c)").bitcast(I32),
+            w_stage[HALF:, 0].rearrange("p i c -> p (i c)").bitcast(I32),
         )
         w_planes = sb("w_planes", [P, 2, R], U8)
         nc.vector.tensor_copy(
             w_planes[:].rearrange("p i (t m) -> p i t m", t=PACK),
-            w_stage[:, 0].rearrange("p i (m t) -> p i t m", t=PACK),
+            w_stage[:, 1].rearrange("p i (m t) -> p i t m", t=PACK),
         )
 
         banks = [psum.tile([P, J], F32, name=f"a_bank{t}") for t in range(PACK)]
         for t in range(PACK):
             cols = slice(P * t, P * (t + 1))
             nc.tensor.matmul_mx(
-                banks[t][:], lhsT=w_w[:, cols].bitcast(E2M1), lhsT_scale=w_planes[:, 0, cols],
-                rhs=tok_w[:].bitcast(E4M3), rhs_scale=tok_s[:], start=True, stop=False,
+                banks[t][:], lhsT=w0_w[:, cols].bitcast(E5M2), lhsT_scale=w_planes[:, 0, cols],
+                rhs=note_w[:].bitcast(E2M1), rhs_scale=note_s[:], start=True, stop=False,
             )
-        a_rows = []
-        for t in range(PACK):
-            cols = slice(P * t, P * (t + 1))
             nc.tensor.matmul_mx(
-                banks[t][:], lhsT=w0_w[:, cols].bitcast(E5M2), lhsT_scale=w_planes[:, 1, cols],
-                rhs=note_w[:].bitcast(E2M1), rhs_scale=note_s[:], start=False, stop=True,
+                banks[t][:], lhsT=w_w[:, cols].bitcast(E2M1), lhsT_scale=w_planes[:, 1, cols],
+                rhs=tok_w[:].bitcast(E4M3), rhs_scale=tok_s[:], start=False, stop=True,
             )
-            a_t = sb(f"a_rows{t}", [P, J], F32)
-            nc.vector.tensor_copy(a_t[:], banks[t][:])
-            a_rows.append(a_t)
+            nc.vector.tensor_copy(a_rows[t][:, :J], banks[t][:])
 
         short_w = gather("short_w", xt_w, list5, U32)
         short_s = gather("short_s", xt_s, list5, U8)
@@ -166,32 +153,39 @@ def tile_list_gatedpool_bank_further_scattered_kernel(
                 rhs=short_w[:].bitcast(E4M3), rhs_scale=short_s[:], start=True, stop=False,
             )
 
+        pooled = sb("pooled", [P, PACK, O], F32)
         hid = sb("hid", [P, O * PACK], BF16)
         hid_w = sb("hid_w", [P, O], U32)
         hid_s = sb("hid_s", [P, O], U8)
-        for h in range(HALVES):
-            part = slice(h * PICKS // 16, (h + 1) * PICKS // 16)
-            gates = sb(f"gates{h}", [P, PACK, PICKS], F32)
-            scaled = sb(f"scaled{h}", [P, PACK, PICKS], F32)
-            h1 = sb(f"h1_{h}", [P, PACK, PICKS], F32)
-            for t in range(PACK):
+        for t in range(PACK):
+            gates = sb(f"gates{t}", [P, I], F32)
+            scaled = sb(f"scaled{t}", [P, I], F32)
+            h1 = sb(f"h1_{t}", [P, I], F32)
+            last = t == PACK - 1
+            width = I // 2 if last else I
+            for i0 in range(0, I, width):
+                picks = slice(i0, i0 + width)
+                part = slice(i0 // 16, (i0 + width) // 16)
+                pools = slice(i0 // 2, (i0 + width) // 2)
                 nc.scalar.activation(
-                    out=gates[:, t, :], in_=a_rows[t][:].indirect(list4[:, part]), func=ACT.Sigmoid,
+                    out=gates[:, picks], in_=a_rows[t][:].indirect(list4[:, part]), func=ACT.Sigmoid,
                     bias=bg_t[:, t : t + 1], scale=sg_t[:, t : t + 1],
                 )
                 nc.scalar.activation(
-                    out=scaled[:, t, :], in_=a_rows[t][:].indirect(list3[:, part]), func=ACT.Copy,
+                    out=scaled[:, picks], in_=a_rows[t][:].indirect(list3[:, part]), func=ACT.Copy,
                     scale=sa_t[:, t : t + 1],
                 )
-                nc.vector.tensor_tensor(h1[:, t, :], scaled[:, t, :], gates[:, t, :], ALU.mult)
-            wide = slice(h * POOLS * PACK, (h + 1) * POOLS * PACK)
-            pools = slice(h * POOLS, (h + 1) * POOLS)
-            nc.vector.tensor_reduce(
-                hid[:, wide].rearrange("p (o t) -> p o t", t=PACK),
-                h1[:].rearrange("p t (o two) -> p o t two", two=2),
-                mybir.AxisListType.X, ALU.max,
-            )
-            nc.vector.quantize_mx(out=hid_w[:, pools].bitcast(E4M3), scales=hid_s[:, pools], in_=hid[:, wide])
+                nc.vector.tensor_tensor(h1[:, picks], scaled[:, picks], gates[:, picks], ALU.mult)
+                nc.vector.tensor_tensor(
+                    pooled[:, t, pools], h1[:, i0 : i0 + width : 2], h1[:, i0 + 1 : i0 + width : 2], ALU.max
+                )
+                if last:
+                    wide = slice(pools.start * PACK, pools.stop * PACK)
+                    nc.vector.tensor_copy(
+                        hid[:, wide].rearrange("p (o t) -> p o t", t=PACK),
+                        pooled[:, :, pools].rearrange("p t o -> p o t"),
+                    )
+                    nc.vector.quantize_mx(out=hid_w[:, pools].bitcast(E4M3), scales=hid_s[:, pools], in_=hid[:, wide])
 
         for b in range(N // P):
             cols = slice(P * b, P * (b + 1))
@@ -199,6 +193,9 @@ def tile_list_gatedpool_bank_further_scattered_kernel(
                 p_banks[b][:], lhsT=wb_w[:, cols].bitcast(E5M2), lhsT_scale=late_planes[:, 1, cols],
                 rhs=hid_w[:].bitcast(E4M3), rhs_scale=hid_s[:], start=False, stop=True,
             )
+        pages = [sb(f"page{b}", [P, E], F32, tag) for b, tag in enumerate(("w_stage", "gates0"))]
+        for page in pages:
+            nc.vector.memset(page[:], 0.0)
         p0 = sb("p0", [P, O], F32)
         p1 = sb("p1", [P, O], F32)
         nc.vector.tensor_copy(p0[:], p_banks[0][:])
@@ -206,4 +203,4 @@ def tile_list_gatedpool_bank_further_scattered_kernel(
         nc.scalar.copy(p1[:], p_banks[1][:])
         nc.scalar.activation(out=pages[1][:].indirect(list6[:]), in_=p1[:], func=ACT.Copy)
         nc.sync.dma_start(out[0:P, :], pages[0][:])
-        nc.sync.dma_start(out[P : 2 * P, :], pages[1][:])
+        nc.scalar.dma_start(out[P : 2 * P, :], pages[1][:])

@@ -43,23 +43,20 @@ def tile_list_gatedpool_bank_further_scattered_kernel(
             nc.sync.dma_start(tile[:], src)
             return tile
 
-        def load_stage(queue, stage, scales, base):
-            rows = scales[0].rearrange("(h q r) c -> q r h c", h=2, q=2)
-            for q in range(2):
-                first = base + 32 * q
-                queue.dma_start(stage[first : first + 4].bitcast(I32), rows[q].bitcast(I32))
+        def load_plane(plane, scales, quadrants):
+            for q in quadrants:
+                nc.sync.dma_start(plane[32 * q : 32 * q + 4].bitcast(I32), scales[0, 4 * q : 4 * q + 4, :].bitcast(I32))
 
         def gather(name, window, lst, dtype):
             dense = sb(name, [P, 16 * lst.shape[1]], dtype)
             nc.vector.tensor_copy(dense[:], window[:].indirect(lst[:]))
             return dense
 
-        xt_stage = sb("xt_stage", [HALF, 2, T], U8)
-        nc.vector.memset(xt_stage[:].bitcast(I32), 0)
+        xt_s = sb("xt_s", [P, T], U8)
         xo_s = sb("xo_s", [P, Z], U8)
-        nc.vector.memset(xo_s[:].bitcast(I32), 0)
-        w_stage = sb("w_stage", [P, 2, 2, R], U8)
-        nc.vector.memset(w_stage[HALF:].bitcast(I32), 0)
+        w_spread = sb("w_spread", [P, 2 * R], U8)
+        for plane in (xt_s, xo_s, w_spread):
+            nc.vector.memset(plane[:].bitcast(I32), 0)
         late_planes = sb("late_planes", [P, 2, N], U8)
         nc.vector.memset(late_planes[:].bitcast(I32), 0)
         a_rows = [sb(f"a_rows{t}", [P, 2 * J], F32) for t in range(PACK)]
@@ -70,17 +67,19 @@ def tile_list_gatedpool_bank_further_scattered_kernel(
         xo_w = sb("xo_w", [P, Z], U16)
         w0_raw = sb("w0_raw", [P, R], U32)
         w_raw = sb("w_raw", [P, R], U16)
-        load_stage(nc.scalar, xt_stage, xt_scales, 0)
+        w_rows = sb("w_rows", [4, 4, 2, R], U8)
+        for i, scales in enumerate((w0_scales, w_scales)):
+            nc.sync.dma_start(
+                w_rows[:, :, i, :].bitcast(I32), scales[0].rearrange("(q r) c -> r q c", q=4).bitcast(I32)
+            )
         list1 = load_list("list1", offs)
         list2 = load_list("list2", offs2)
         nc.sync.dma_start(xt_w[:].bitcast(I32), fp8_words(xt_words))
         nc.sync.dma_start(xo_w[:].bitcast(I32), xo_words[0].bitcast(I32))
-        nc.sync.dma_start(w0_raw[:].bitcast(I32), fp8_words(w0_words))
+        load_plane(xt_s, xt_scales, range(4))
         nc.sync.dma_start(w_raw[:].bitcast(I32), w_words[0].bitcast(I32))
-        for q in range(4):
-            nc.sync.dma_start(xo_s[32 * q : 32 * q + 4, :].bitcast(I32), xo_scales[0, 4 * q : 4 * q + 4, :].bitcast(I32))
-        for i, scales in enumerate((w0_scales, w_scales)):
-            load_stage(nc.sync, w_stage[:, :, i, :], scales, HALF)
+        nc.sync.dma_start(w0_raw[:].bitcast(I32), fp8_words(w0_words))
+        load_plane(xo_s, xo_scales, range(4))
         list4 = load_list("list4", offs4)
         list3 = load_list("list3", offs3)
 
@@ -97,49 +96,42 @@ def tile_list_gatedpool_bank_further_scattered_kernel(
         nc.sync.dma_start(ws_w[:].bitcast(I32), fp8_words(ws_words))
         nc.sync.dma_start(wb_w[:].bitcast(I32), fp8_words(wb_words))
         for i, scales in enumerate((ws_scales, wb_scales)):
-            for q in range(4):
-                nc.sync.dma_start(
-                    late_planes[32 * q : 32 * q + 4, i, :].bitcast(I32), scales[0, 4 * q : 4 * q + 4, :].bitcast(I32)
-                )
+            load_plane(late_planes[:, i, :], scales, range(4))
         list6 = load_list("list6", offs6)
 
+        w_words_of = w_rows[:].rearrange("p q i c -> p q (i c)")
+        for q in range(4):
+            nc.vector.tensor_copy(w_spread[32 * q : 32 * q + 4, :].bitcast(I32), w_words_of[:, q, :].bitcast(I32))
+        w_planes = sb("w_planes", [P, 2, R], U8)
+        nc.vector.tensor_copy(
+            w_planes[:].rearrange("p i (t m) -> p i t m", t=PACK),
+            w_spread[:].rearrange("p (i m t) -> p i t m", i=2, t=PACK),
+        )
         tok_w = gather("tok_w", xt_w, list1, U32)
         note_w = gather("note_w", xo_w, list2, U16)
-        xt_s = sb("xt_s", [P, T], U8)
-        for h in range(2):
-            nc.vector.tensor_copy(xt_s[HALF * h : HALF * (h + 1), :].bitcast(I32), xt_stage[:, h, :].bitcast(I32))
         tok_s = gather("tok_s", xt_s, list1, U8)
         note_s = gather("note_s", xo_s, list2, U8)
 
         w0_w = sb("w0_w", [P, R], U32)
         w_w = sb("w_w", [P, R], U16)
         nc.scalar.copy(
-            w0_w[:].rearrange("p (t c i) -> p c t i", t=PACK, i=4),
-            w0_raw[:].rearrange("p (c i t) -> p c t i", t=PACK, i=4),
-        )
-        nc.scalar.copy(
             w_w[:].rearrange("p (t m) -> p t m", t=PACK), w_raw[:].rearrange("p (m t) -> p t m", t=PACK)
         )
-        nc.vector.tensor_copy(
-            w_stage[:HALF, 1].rearrange("p i c -> p (i c)").bitcast(I32),
-            w_stage[HALF:, 0].rearrange("p i c -> p (i c)").bitcast(I32),
-        )
-        w_planes = sb("w_planes", [P, 2, R], U8)
-        nc.vector.tensor_copy(
-            w_planes[:].rearrange("p i (t m) -> p i t m", t=PACK),
-            w_stage[:, 1].rearrange("p i (m t) -> p i t m", t=PACK),
+        nc.scalar.copy(
+            w0_w[:].rearrange("p (t c i) -> p c t i", t=PACK, i=4),
+            w0_raw[:].rearrange("p (c i t) -> p c t i", t=PACK, i=4),
         )
 
         banks = [psum.tile([P, J], F32, name=f"a_bank{t}") for t in range(PACK)]
         for t in range(PACK):
             cols = slice(P * t, P * (t + 1))
             nc.tensor.matmul_mx(
-                banks[t][:], lhsT=w0_w[:, cols].bitcast(E5M2), lhsT_scale=w_planes[:, 0, cols],
-                rhs=note_w[:].bitcast(E2M1), rhs_scale=note_s[:], start=True, stop=False,
+                banks[t][:], lhsT=w_w[:, cols].bitcast(E2M1), lhsT_scale=w_planes[:, 1, cols],
+                rhs=tok_w[:].bitcast(E4M3), rhs_scale=tok_s[:], start=True, stop=False,
             )
             nc.tensor.matmul_mx(
-                banks[t][:], lhsT=w_w[:, cols].bitcast(E2M1), lhsT_scale=w_planes[:, 1, cols],
-                rhs=tok_w[:].bitcast(E4M3), rhs_scale=tok_s[:], start=False, stop=True,
+                banks[t][:], lhsT=w0_w[:, cols].bitcast(E5M2), lhsT_scale=w_planes[:, 0, cols],
+                rhs=note_w[:].bitcast(E2M1), rhs_scale=note_s[:], start=False, stop=True,
             )
             nc.vector.tensor_copy(a_rows[t][:, :J], banks[t][:])
 
@@ -193,7 +185,7 @@ def tile_list_gatedpool_bank_further_scattered_kernel(
                 p_banks[b][:], lhsT=wb_w[:, cols].bitcast(E5M2), lhsT_scale=late_planes[:, 1, cols],
                 rhs=hid_w[:].bitcast(E4M3), rhs_scale=hid_s[:], start=False, stop=True,
             )
-        pages = [sb(f"page{b}", [P, E], F32, tag) for b, tag in enumerate(("w_stage", "gates0"))]
+        pages = [sb(f"page{b}", [P, E], F32, tag) for b, tag in enumerate(("page0", "gates0"))]
         for page in pages:
             nc.vector.memset(page[:], 0.0)
         p0 = sb("p0", [P, O], F32)

@@ -47,8 +47,13 @@ def tile_list_gatedpool_bank_further_scattered_kernel(
             for q in quadrants:
                 nc.sync.dma_start(plane[32 * q : 32 * q + 4].bitcast(I32), scales[0, 4 * q : 4 * q + 4, :].bitcast(I32))
 
-        def gather(name, window, lst, dtype):
-            dense = sb(name, [P, 16 * lst.shape[1]], dtype)
+        def load_rowvals(queue, name, src):
+            tile = keep.tile([P, PACK], F32, name=name)
+            queue.dma_start(tile[:], src.rearrange("(p t) one -> p (t one)", t=PACK))
+            return tile
+
+        def gather(name, window, lst, dtype, tag=None):
+            dense = sb(name, [P, 16 * lst.shape[1]], dtype, tag)
             nc.vector.tensor_copy(dense[:], window[:].indirect(lst[:]))
             return dense
 
@@ -74,21 +79,18 @@ def tile_list_gatedpool_bank_further_scattered_kernel(
             )
         list1 = load_list("list1", offs)
         list2 = load_list("list2", offs2)
+        nc.gpsimd.dma_start(w_raw[:].bitcast(I32), w_words[0].bitcast(I32))
+        nc.gpsimd.dma_start(w0_raw[:].bitcast(I32), fp8_words(w0_words))
+        load_plane(xt_s, xt_scales, range(2))
         nc.sync.dma_start(xt_w[:].bitcast(I32), fp8_words(xt_words))
         nc.sync.dma_start(xo_w[:].bitcast(I32), xo_words[0].bitcast(I32))
-        load_plane(xt_s, xt_scales, range(4))
-        nc.sync.dma_start(w_raw[:].bitcast(I32), w_words[0].bitcast(I32))
-        nc.sync.dma_start(w0_raw[:].bitcast(I32), fp8_words(w0_words))
+        load_plane(xt_s, xt_scales, range(2, 4))
         load_plane(xo_s, xo_scales, range(4))
+        sg_t = load_rowvals(nc.gpsimd, "sg_t", sg)
         list4 = load_list("list4", offs4)
+        bg_t = load_rowvals(nc.sync, "bg_t", bg)
         list3 = load_list("list3", offs3)
-
-        rowvals = []
-        for name, src in (("sg_t", sg), ("bg_t", bg), ("sa_t", sa)):
-            tile = keep.tile([P, PACK], F32, name=name)
-            nc.gpsimd.dma_start(tile[:], src.rearrange("(p t) one -> p (t one)", t=PACK))
-            rowvals.append(tile)
-        sg_t, bg_t, sa_t = rowvals
+        sa_t = load_rowvals(nc.sync, "sa_t", sa)
 
         list5 = load_list("list5", offs5)
         ws_w = sb("ws_w", [P, N], U32)
@@ -122,21 +124,21 @@ def tile_list_gatedpool_bank_further_scattered_kernel(
             w0_raw[:].rearrange("p (c i t) -> p c t i", t=PACK, i=4),
         )
 
-        banks = [psum.tile([P, J], F32, name=f"a_bank{t}") for t in range(PACK)]
         for t in range(PACK):
+            bank = psum.tile([P, J], F32, name=f"a_bank{t}", tag=f"a_bank{t % 2}")
             cols = slice(P * t, P * (t + 1))
             nc.tensor.matmul_mx(
-                banks[t][:], lhsT=w_w[:, cols].bitcast(E2M1), lhsT_scale=w_planes[:, 1, cols],
+                bank[:], lhsT=w_w[:, cols].bitcast(E2M1), lhsT_scale=w_planes[:, 1, cols],
                 rhs=tok_w[:].bitcast(E4M3), rhs_scale=tok_s[:], start=True, stop=False,
             )
             nc.tensor.matmul_mx(
-                banks[t][:], lhsT=w0_w[:, cols].bitcast(E5M2), lhsT_scale=w_planes[:, 0, cols],
+                bank[:], lhsT=w0_w[:, cols].bitcast(E5M2), lhsT_scale=w_planes[:, 0, cols],
                 rhs=note_w[:].bitcast(E2M1), rhs_scale=note_s[:], start=False, stop=True,
             )
-            nc.vector.tensor_copy(a_rows[t][:, :J], banks[t][:])
+            nc.vector.tensor_copy(a_rows[t][:, :J], bank[:])
 
-        short_w = gather("short_w", xt_w, list5, U32)
-        short_s = gather("short_s", xt_s, list5, U8)
+        short_w = gather("short_w", xt_w, list5, U32, "tok_w")
+        short_s = gather("short_s", xt_s, list5, U8, "tok_s")
         p_banks = [psum.tile([P, O], F32, name=f"p_bank{b}") for b in range(N // P)]
         for b in range(N // P):
             cols = slice(P * b, P * (b + 1))
@@ -185,9 +187,9 @@ def tile_list_gatedpool_bank_further_scattered_kernel(
                 p_banks[b][:], lhsT=wb_w[:, cols].bitcast(E5M2), lhsT_scale=late_planes[:, 1, cols],
                 rhs=hid_w[:].bitcast(E4M3), rhs_scale=hid_s[:], start=False, stop=True,
             )
-        pages = [sb(f"page{b}", [P, E], F32, tag) for b, tag in enumerate(("page0", "gates0"))]
+        pages = [sb(f"page{b}", [P, E], F32, tag) for b, tag in enumerate(("w_w", "w0_w"))]
         for page in pages:
-            nc.vector.memset(page[:], 0.0)
+            nc.gpsimd.memset(page[:], 0.0)
         p0 = sb("p0", [P, O], F32)
         p1 = sb("p1", [P, O], F32)
         nc.vector.tensor_copy(p0[:], p_banks[0][:])

from contextlib import ExitStack

import concourse.mybir as mybir

K, T, J, R, F, Z, I, O, N, E = 512, 1024, 256, 512, 512, 1024, 256, 128, 256, 1024
FLOPS = 2 * (K * R * J + F * R * J + R * N * O + K * N * O)

F32 = mybir.dt.float32
BF16 = mybir.dt.bfloat16
I32 = mybir.dt.int32
U32 = mybir.dt.uint32
U16 = mybir.dt.uint16
U8 = mybir.dt.uint8
E4M3 = mybir.dt.float8_e4m3fn_x4
E5M2 = mybir.dt.float8_e5m2_x4
E2M1 = mybir.dt.float4_e2m1fn_x4
ACT = mybir.ActivationFunctionType
ALU = mybir.AluOpType

P = 128
PACK = 4
HALF = P // 2


def fp8_words(words):
    return words[0].rearrange("p c b -> p (c b)").bitcast(I32)


def tile_list_gatedpool_bank_further_scattered_kernel(
    tc, xt_words, xt_scales, xo_words, xo_scales, w_words, w_scales, w0_words, w0_scales, sa, sg, bg,
    wb_words, wb_scales, ws_words, ws_scales, offs, offs2, offs3, offs4, offs5, offs6, out,
):
    nc = tc.nc
    with ExitStack() as ctx:
        keep = ctx.enter_context(tc.tile_pool(name="keep", bufs=1))
        psum = ctx.enter_context(tc.psum_pool(name="psum", bufs=1))

        def sb(name, shape, dtype, tag=None):
            return keep.tile(shape, dtype, name=name, tag=tag or name, align_bytes=64)

        def load_list(name, src):
            tile = keep.tile(list(src.shape), U16, name=name)
            nc.sync.dma_start(tile[:], src)
            return tile

        def load_plane(plane, scales, quadrants):
            for q in quadrants:
                nc.sync.dma_start(plane[32 * q : 32 * q + 4].bitcast(I32), scales[0, 4 * q : 4 * q + 4, :].bitcast(I32))

        def load_rowvals(queue, name, src):
            tile = keep.tile([P, PACK], F32, name=name)
            queue.dma_start(tile[:], src.rearrange("(p t) one -> p (t one)", t=PACK))
            return tile

        def gather(name, window, lst, dtype, tag=None):
            dense = sb(name, [P, 16 * lst.shape[1]], dtype, tag)
            nc.vector.tensor_copy(dense[:], window[:].indirect(lst[:]))
            return dense

        xt_s = sb("xt_s", [P, T], U8)
        xo_s = sb("xo_s", [P, Z], U8)
        w_spread = sb("w_spread", [P, 2 * R], U8)
        for plane in (xt_s, xo_s, w_spread):
            nc.vector.memset(plane[:].bitcast(I32), 0)
        late_planes = sb("late_planes", [P, 2, N], U8)
        nc.vector.memset(late_planes[:].bitcast(I32), 0)
        a_rows = [sb(f"a_rows{t}", [P, 2 * J], F32) for t in range(PACK)]
        for a_t in a_rows:
            nc.vector.memset(a_t[:, J:], 0.0)

        xt_w = sb("xt_w", [P, T], U32)
        xo_w = sb("xo_w", [P, Z], U16)
        w0_raw = sb("w0_raw", [P, R], U32)
        w_raw = sb("w_raw", [P, R], U16)
        w_rows = sb("w_rows", [4, 4, 2, R], U8)
        for i, scales in enumerate((w0_scales, w_scales)):
            nc.sync.dma_start(
                w_rows[:, :, i, :].bitcast(I32), scales[0].rearrange("(q r) c -> r q c", q=4).bitcast(I32)
            )
        list1 = load_list("list1", offs)
        list2 = load_list("list2", offs2)
        nc.gpsimd.dma_start(w_raw[:].bitcast(I32), w_words[0].bitcast(I32))
        nc.gpsimd.dma_start(w0_raw[:].bitcast(I32), fp8_words(w0_words))
        load_plane(xt_s, xt_scales, range(2))
        nc.sync.dma_start(xt_w[:].bitcast(I32), fp8_words(xt_words))
        nc.sync.dma_start(xo_w[:].bitcast(I32), xo_words[0].bitcast(I32))
        load_plane(xt_s, xt_scales, range(2, 4))
        load_plane(xo_s, xo_scales, range(4))
        sg_t = load_rowvals(nc.gpsimd, "sg_t", sg)
        list4 = load_list("list4", offs4)
        bg_t = load_rowvals(nc.sync, "bg_t", bg)
        list3 = load_list("list3", offs3)
        sa_t = load_rowvals(nc.sync, "sa_t", sa)

        list5 = load_list("list5", offs5)
        ws_w = sb("ws_w", [P, N], U32)
        wb_w = sb("wb_w", [P, N], U32)
        nc.sync.dma_start(ws_w[:].bitcast(I32), fp8_words(ws_words))
        nc.sync.dma_start(wb_w[:].bitcast(I32), fp8_words(wb_words))
        for i, scales in enumerate((ws_scales, wb_scales)):
            load_plane(late_planes[:, i, :], scales, range(4))
        list6 = load_list("list6", offs6)

        w_words_of = w_rows[:].rearrange("p q i c -> p q (i c)")
        for q in range(4):
            nc.vector.tensor_copy(w_spread[32 * q : 32 * q + 4, :].bitcast(I32), w_words_of[:, q, :].bitcast(I32))
        w_planes = sb("w_planes", [P, 2, R], U8)
        nc.vector.tensor_copy(
            w_planes[:].rearrange("p i (t m) -> p i t m", t=PACK),
            w_spread[:].rearrange("p (i m t) -> p i t m", i=2, t=PACK),
        )
        tok_w = gather("tok_w", xt_w, list1, U32)
        note_w = gather("note_w", xo_w, list2, U16)
        tok_s = gather("tok_s", xt_s, list1, U8)
        note_s = gather("note_s", xo_s, list2, U8)

        w0_w = sb("w0_w", [P, R], U32)
        w_w = sb("w_w", [P, R], U16)
        nc.scalar.copy(
            w_w[:].rearrange("p (t m) -> p t m", t=PACK), w_raw[:].rearrange("p (m t) -> p t m", t=PACK)
        )
        nc.scalar.copy(
            w0_w[:].rearrange("p (t c i) -> p c t i", t=PACK, i=4),
            w0_raw[:].rearrange("p (c i t) -> p c t i", t=PACK, i=4),
        )

        for t in range(PACK):
            bank = psum.tile([P, J], F32, name=f"a_bank{t}", tag=f"a_bank{t % 2}")
            cols = slice(P * t, P * (t + 1))
            nc.tensor.matmul_mx(
                bank[:], lhsT=w_w[:, cols].bitcast(E2M1), lhsT_scale=w_planes[:, 1, cols],
                rhs=tok_w[:].bitcast(E4M3), rhs_scale=tok_s[:], start=True, stop=False,
            )
            nc.tensor.matmul_mx(
                bank[:], lhsT=w0_w[:, cols].bitcast(E5M2), lhsT_scale=w_planes[:, 0, cols],
                rhs=note_w[:].bitcast(E2M1), rhs_scale=note_s[:], start=False, stop=True,
            )
            nc.vector.tensor_copy(a_rows[t][:, :J], bank[:])

        short_w = gather("short_w", xt_w, list5, U32, "tok_w")
        short_s = gather("short_s", xt_s, list5, U8, "tok_s")
        p_banks = [psum.tile([P, O], F32, name=f"p_bank{b}") for b in range(N // P)]
        for b in range(N // P):
            cols = slice(P * b, P * (b + 1))
            nc.tensor.matmul_mx(
                p_banks[b][:], lhsT=ws_w[:, cols].bitcast(E5M2), lhsT_scale=late_planes[:, 0, cols],
                rhs=short_w[:].bitcast(E4M3), rhs_scale=short_s[:], start=True, stop=False,
            )

        pooled = sb("pooled", [P, PACK, O], F32)
        hid = sb("hid", [P, O * PACK], BF16)
        hid_w = sb("hid_w", [P, O], U32)
        hid_s = sb("hid_s", [P, O], U8)
        for t in range(PACK):
            gates = sb(f"gates{t}", [P, I], F32)
            scaled = sb(f"scaled{t}", [P, I], F32)
            h1 = sb(f"h1_{t}", [P, I], F32)
            last = t == PACK - 1
            width = I // 2 if last else I
            for i0 in range(0, I, width):
                picks = slice(i0, i0 + width)
                part = slice(i0 // 16, (i0 + width) // 16)
                pools = slice(i0 // 2, (i0 + width) // 2)
                nc.scalar.activation(
                    out=gates[:, picks], in_=a_rows[t][:].indirect(list4[:, part]), func=ACT.Sigmoid,
                    bias=bg_t[:, t : t + 1], scale=sg_t[:, t : t + 1],
                )
                nc.scalar.activation(
                    out=scaled[:, picks], in_=a_rows[t][:].indirect(list3[:, part]), func=ACT.Copy,
                    scale=sa_t[:, t : t + 1],
                )
                nc.vector.tensor_tensor(h1[:, picks], scaled[:, picks], gates[:, picks], ALU.mult)
                nc.vector.tensor_tensor(
                    pooled[:, t, pools], h1[:, i0 : i0 + width : 2], h1[:, i0 + 1 : i0 + width : 2], ALU.max
                )
                if last:
                    wide = slice(pools.start * PACK, pools.stop * PACK)
                    nc.vector.tensor_copy(
                        hid[:, wide].rearrange("p (o t) -> p o t", t=PACK),
                        pooled[:, :, pools].rearrange("p t o -> p o t"),
                    )
                    nc.vector.quantize_mx(out=hid_w[:, pools].bitcast(E4M3), scales=hid_s[:, pools], in_=hid[:, wide])

        for b in range(N // P):
            cols = slice(P * b, P * (b + 1))
            nc.tensor.matmul_mx(
                p_banks[b][:], lhsT=wb_w[:, cols].bitcast(E5M2), lhsT_scale=late_planes[:, 1, cols],
                rhs=hid_w[:].bitcast(E4M3), rhs_scale=hid_s[:], start=False, stop=True,
            )
        pages = [sb(f"page{b}", [P, E], F32, tag) for b, tag in enumerate(("w_w", "w0_w"))]
        for page in pages:
            nc.gpsimd.memset(page[:], 0.0)
        p0 = sb("p0", [P, O], F32)
        p1 = sb("p1", [P, O], F32)
        nc.vector.tensor_copy(p0[:], p_banks[0][:])
        nc.vector.tensor_copy(pages[0][:].indirect(list6[:]), p0[:])
        nc.scalar.copy(p1[:], p_banks[1][:])
        nc.scalar.activation(out=pages[1][:].indirect(list6[:]), in_=p1[:], func=ACT.Copy)
        nc.sync.dma_start(out[0:P, :], pages[0][:])
        nc.scalar.dma_start(out[P : 2 * P, :], pages[1][:])
